import numpy as np, ml_dtypes
CORES = [30,158,46,174,86,214]
N = 6
import mx_ref
BF = ml_dtypes.bfloat16
def f(rng, *shape):
    return mx_ref.flush((rng.standard_normal(shape, dtype=np.float32) * np.exp2(rng.integers(-2, 3, shape[:-1] + (1,)))).astype(BF))
def wide(rng, *shape, cols=0):
    v = rng.standard_normal(shape, dtype=np.float32) * np.exp2(rng.integers(-12, 13, shape)).astype(np.float32)
    if cols: v *= np.repeat(np.exp2(rng.integers(-cols, cols + 1, shape[:-2] + (1, shape[-1] // 4))) * (rng.random(shape[:-2] + (1, shape[-1] // 4)) > 0.0625), 4, axis=-1).astype(np.float32)
    return mx_ref.flush(v.astype(BF))
PG, PW = 8, 64
def bare(d):
    d["sm"][:, :, 4 * PG:] = 0; d["gs"][:, :, 8:] = 0
    return d
def sizes(rng, d):
    for n in ("sm", "gs"): d[n] = mx_ref.flush((d[n].astype(np.float32) * np.exp2(rng.integers(-12, 13, (N, 1, 1))).astype(np.float32)).astype(BF))
    return d
def setup_inputs(rng):
    return bare({"pg": f(rng, N, 128 * PG, 4 * PW), "sm": f(rng, N, 128, 512), "gs": f(rng, N, 128, 512), "qw": f(rng, N, 128, 1024)})
def setup_inputs_ties(rng):
    d = setup_inputs(rng); v = d["sm"].reshape(N, 128, 128, 4).copy()
    for q in range(N):
        k = rng.integers(PG // 4 + 1, PG // 2 + 1); p = rng.permutation(PG)
        v[q][:, p[k:]] = v[q][:, p[np.arange(k, PG) % k]]
    d["sm"] = v.reshape(N, 128, 512)
    d = sizes(rng, d)
    for r in rng.permutation(N)[:2]: d["gs"][r][:, 4:8] = 0
    return d
def setup_inputs_last(rng):
    d = setup_inputs(rng); c = f(rng, 128, 4)
    for r in range(N):
        j = rng.integers(0, 2)
        d["gs"][r][:, 4 * j:4 * j + 4] = c
        d["sm"][r][:, 4 * PG - 4:4 * PG] = (c.astype(np.float32) * 2).astype(BF)
    return d
def setup_inputs_alike(rng):
    d = setup_inputs(rng); d["gs"] = np.stack([d["gs"][0]] * N); return d
def setup_inputs_below(rng):
    d = setup_inputs(rng)
    d["gs"] = np.abs(d["gs"].astype(np.float32)).astype(BF)
    d["sm"] = (-np.abs(d["sm"].astype(np.float32))).astype(BF)
    return bare(sizes(rng, d))
def setup_inputs_spread(rng):
    d = setup_inputs(rng); d["pg"] = wide(rng, N, 128 * PG, 4 * PW); d["sm"] = wide(rng, N, 128, 512); d["gs"] = wide(rng, N, 128, 512)
    return bare(d)
def check_inputs(d):
    b = []
    for r in range(N):
        if d["sm"][r][:, 4 * PG:].astype(np.float32).any(): b.append("sm")
        if d["gs"][r][:, 8:].astype(np.float32).any(): b.append("gs")
    return b
def reference(pg, sm, gs, qw):
    S = [mx_ref.quantize(t) for t in sm]; G = [mx_ref.quantize(t) for t in gs]
    y = np.zeros((N, 128, 2 * N * PW), np.float32); ch = np.zeros((N, 2, N), np.float32)
    for r in range(N):
        W = [mx_ref.quantize(qw[r][:, 512 * j:512 * j + 512]) for j in range(2)]
        for q in range(N):
            score = mx_ref.matmul(S[q], G[r])
            for j in range(2):
                c = int(np.argmax(score[:PG, j]))
                k = PW * (j * N + q)
                y[r][:, k:k + PW] = mx_ref.matmul(W[j], mx_ref.quantize(pg[q][128 * c:128 * c + 128]))
                ch[r, j, q] = c
    return {"y": y, "ch": ch}

@@ -1,0 +1,265 @@
+from concourse.bass import DstId, RemoteDMATransfer
+from concourse.mybir import dt, AluOpType, ActivationFunctionType
+
+U8 = dt.uint8
+COPY = ActivationFunctionType.Copy
+NR = 6
+NO = NR - 1
+
+SCRATCH = {
+    "gt": ("sbuf", [128, 512], "bfloat16"),
+    "st": ("sbuf", [128, 512], "bfloat16"),
+    "pgt": ("sbuf", [128, 2048], "bfloat16"),
+    "wt": ("sbuf", [128, 1024], "bfloat16"),
+    "gq": ("sbuf", [128, 144], "float8_e4m3fn_x4"),
+    "gp": ("sbuf", [128, 144], "uint8"),
+    "sq": ("sbuf", [128, 128], "float8_e4m3fn_x4"),
+    "sp": ("sbuf", [128, 128], "uint8"),
+    "wq": ("sbuf", [128, 256], "float8_e4m3fn_x4"),
+    "wp": ("sbuf", [128, 256], "uint8"),
+    "pq": ("sbuf", [128, 512], "float8_e4m3fn_x4"),
+    "pp": ("sbuf", [128, 512], "uint8"),
+    "hb": ("sbuf", [128, 2560], "bfloat16"),
+    "hq": ("sbuf", [128, 640], "float8_e4m3fn_x4"),
+    "hp": ("sbuf", [128, 640], "uint8"),
+    "lq": ("sbuf", [128, 640], "float8_e4m3fn_x4"),
+    "lp": ("sbuf", [128, 640], "uint8"),
+    "ow": ("sbuf", [128, 1024], "float32"),
+    "yb": ("sbuf", [128, 768], "float32"),
+    "sc": ("sbuf", [128, 32], "float32"),
+    "pm": ("sbuf", [128, 8], "float32"),
+    "lt": ("sbuf", [128, 64], "float32"),
+    "zz": ("sbuf", [128, 40], "float32"),
+    "bb": ("sbuf", [128, 64], "float32"),
+    "bt": ("sbuf", [128, 32], "float32"),
+    "i0": ("sbuf", [128, 16], "int32"),
+    "i1": ("sbuf", [128, 16], "int32"),
+    "i2": ("sbuf", [128, 16], "int32"),
+    "i3": ("sbuf", [128, 16], "float32"),
+    "if256": ("sbuf", [128, 16], "float32"),
+    "if64": ("sbuf", [128, 4], "float32"),
+    "off": ("sbuf", [128, 160], "uint16"),
+    "offo": ("sbuf", [128, 8], "uint16"),
+    "chs": ("sbuf", [128, 12], "float32"),
+    "cho": ("sbuf", [128, 12], "float32"),
+    "chd": ("dram", [640, 2], "float32"),
+    "dd": ("dram", [128, 2], "float32"),
+    "ps": ("psum", [128, 4096], "float32"),
+}
+SEMAPHORES = (["gsl", "sml", "qwl", "pgl", "mg", "ms", "ml", "mz", "ii", "jj", "k2", "k3", "k4", "k5",
+               "cs", "qg", "qs", "qw", "qp", "sc", "v1", "v2", "v3", "v4", "v5", "oo", "go",
+               "gsa", "lg", "lpg", "lch", "dch", "cha", "chl", "chv", "chst", "yst", "kk"]
+              + ["of%d%d" % (t, j) for t in range(NO) for j in range(2)]
+              + ["gv%d" % t for t in range(NO)] + ["gz%d" % t for t in range(NO)]
+              + ["hq%d" % t for t in range(NO)]
+              + ["pa%d" % t for t in range(NO)]
+              + ["mm%d%d" % (t, j) for t in range(NO) for j in range(2)]
+              + ["cp%d%d" % (t, j) for t in range(NO) for j in range(2)]
+              + ["om%d" % j for j in range(2)] + ["oc%d" % j for j in range(2)] + ["oy%d" % j for j in range(2)])
+
+
+def rank_program(g, core, T, topo):
+    r = T.rank_of(core)
+    if r is None:
+        return
+    S = T.sem
+    V, A, P, Y = g.vector, g.scalar, g.tensor, g.sync
+    others = [q for q in range(NR) if q != r]
+    slot = lambda q, at: q - (q > at)
+    order = [(r + 1 + t) % NR for t in range(NO)]
+    come = [(r - 1 - t) % NR for t in range(NO)]
+    eng = lambda d: topo.mask(core, T.cores[d])
+    allmask = eng(others[0])
+    for d in others:
+        allmask &= eng(d)
+    count = bin(allmask).count("1")
+
+    def did(d):
+        rid, pid = topo.addr(T.cores[d], core)
+        return DstId(rid=rid, pnc=pid)
+
+    Y.dma_start(T.gt[:, 0:8], T.gs[:, 0:8]).then_inc(S.gsl, 16)
+    A.dma_start(T.st[:, 0:32], T.sm[:, 0:32]).then_inc(S.sml, 16)
+    A.dma_start(T.wt[:], T.qw[:]).then_inc(S.qwl, 16)
+    for m in range(8):
+        (Y if m % 2 == 0 else A).dma_start(T.pgt[:, 256 * m:256 * m + 256], T.pg[128 * m:128 * m + 128, :]).then_inc(S.pgl, 16)
+
+    g.iota(T.i0[:], [[0, 16]], 0, 1).then_inc(S.ii, 1)
+    g.iota(T.i1[:], [[16, 16]], 0, 0).then_inc(S.jj, 1)
+    V.memset(T.gt[:, 8:512], 0.0).then_inc(S.mg, 1)
+    V.memset(T.st[:, 32:512], 0.0).then_inc(S.ms, 1)
+    V.memset(T.lt[:, 32:64], 0.0).then_inc(S.ml, 1)
+    V.memset(T.zz[:], 0.0).then_inc(S.mz, 1)
+
+    V.wait_ge(S.mg, 1)
+    V.wait_ge(S.gsl, 16)
+    V.quantize_mx(T.gq[:, 16:144], T.gp[:, 16:144], T.gt[:]).then_inc(S.qg, 1)
+    g.wait_ge(S.qg, 1)
+    ids = [did(d) for d in others]
+    at = [6 + 2 * slot(r, d) for d in others]
+    g.remote_dma_fused([RemoteDMATransfer(dst_ids=ids, dma_engine_mask=allmask, remote_sem=S.gsa,
+                                          srcs=[T.gq[:, 16:18].bitcast(U8)],
+                                          dsts=[T.gq[:, a:a + 2].bitcast(U8) for a in at])], local_sem=S.lg)
+    g.remote_dma_fused([RemoteDMATransfer(dst_ids=ids, dma_engine_mask=allmask, remote_sem=S.gsa,
+                                          srcs=[T.gp[:, 16:18]],
+                                          dsts=[T.gp[:, a:a + 2] for a in at])], local_sem=S.lg)
+
+    V.wait_ge(S.ii, 1)
+    V.tensor_scalar(T.i2[:], T.i0[:], 15, None, AluOpType.bitwise_and).then_inc(S.k2, 1)
+    V.wait_ge(S.k2, 1)
+    V.wait_ge(S.jj, 1)
+    V.tensor_tensor(T.i3[:], T.i2[:], T.i1[:], AluOpType.add).then_inc(S.k3, 1)
+    V.wait_ge(S.k3, 1)
+    V.tensor_scalar(T.if256[:], T.i3[:], 1.0 / 256, None, AluOpType.mult).then_inc(S.k4, 1)
+    V.tensor_scalar(T.if64[:], T.i3[:, 0:4], 1.0 / 64, None, AluOpType.mult).then_inc(S.k5, 1)
+
+    V.wait_ge(S.ms, 1)
+    V.wait_ge(S.sml, 16)
+    for a in range(1, 4):
+        V.tensor_copy(T.st[:, 128 * a:128 * a + 32], T.st[:, 0:32]).then_inc(S.cs, 1)
+    V.wait_ge(S.cs, 3)
+    V.quantize_mx(T.sq[:], T.sp[:], T.st[:]).then_inc(S.qs, 1)
+    V.wait_ge(S.qwl, 16)
+    V.quantize_mx(T.wq[:], T.wp[:], T.wt[:]).then_inc(S.qw, 1)
+
+    P.wait_ge(S.qs, 1)
+    P.wait_ge(S.qg, 1)
+    P.wait_ge(S.gsa, 2 * count * NO)
+    P.matmul_mx(T.ps[:, 0:138], T.sq[:], T.sp[:], T.gq[:, 6:144], T.gp[:, 6:144], True, True).then_inc(S.sc, 1)
+
+    V.wait_ge(S.sc, 1)
+    V.transpose(T["sc"][:], T.ps[:, 0:32]).then_inc(S.v1, 1)
+    V.wait_ge(S.v1, 1)
+    V.tensor_tensor_scan(T["pm"][:], T["sc"][:, 0:8], T["sc"][:, 0:8], T["sc"][:, 0:1],
+                         AluOpType.max, AluOpType.max).then_inc(S.v2, 1)
+    V.wait_ge(S.v2, 1)
+    V.tensor_scalar(T["lt"][:, 24:32], T["pm"][:], T["pm"][:, 7:8], None, AluOpType.is_lt).then_inc(S.v3, 1)
+    V.wait_ge(S.ml, 1)
+    V.wait_ge(S.mz, 1)
+    V.wait_ge(S.v3, 1)
+    V.tensor_tensor_scan(T.bb[:, 24:64], T["lt"][:, 24:64], T.zz[:], 0.0,
+                         AluOpType.add, AluOpType.add).then_inc(S.v4, 1)
+    V.wait_ge(S.v4, 1)
+    V.transpose(T.bt[:], T.bb[:, 32:64]).then_inc(S.v5, 1)
+
+    V.wait_ge(S.k4, 1)
+    V.wait_ge(S.v5, 1)
+    win = T.pgt[:, 0:2048]
+    both = (3,)
+
+    def offsets(t):
+        for j in (1, 0):
+            c = 2 * slot(order[t], r) + j
+            k = 32 * t + 16 * j
+            V.tensor_scalar(T.off[:, k:k + 16], T.if256[:], T.bt[:, c:c + 1], 256.0,
+                            AluOpType.add, AluOpType.mult).then_inc(S["of%d%d" % (t, j)], 1)
+
+    offsets(0)
+    for t in range(NO):
+        d = order[t]
+        k, h = 32 * t, 512 * t
+        if t == 0:
+            A.wait_ge(S.pgl, 128)
+            V.wait_ge(S.pgl, 128)
+        A.wait_ge(S["of%d1" % t], 1)
+        if t in both:
+            A.wait_ge(S["of%d0" % t], 1)
+            A.activation(T.hb[:, h:h + 512], win.indirect(T.off[:, k:k + 32]), COPY).then_inc(S["gz%d" % t], 1)
+        else:
+            A.activation(T.hb[:, h + 256:h + 512], win.indirect(T.off[:, k + 16:k + 32]), COPY).then_inc(S["gz%d" % t], 1)
+            V.wait_ge(S["of%d0" % t], 1)
+            V.tensor_copy(T.hb[:, h:h + 256], win.indirect(T.off[:, k:k + 16])).then_inc(S["gv%d" % t], 1)
+        if 0 < t < NO - 1:
+            offsets(t + 1)
+        if t not in both:
+            V.wait_ge(S["gv%d" % t], 1)
+        V.wait_ge(S["gz%d" % t], 1)
+        V.quantize_mx(T.hq[:, 128 * t:128 * t + 128], T.hp[:, 128 * t:128 * t + 128],
+                      T.hb[:, h:h + 512]).then_inc(S["hq%d" % t], 1)
+        if t == 0:
+            offsets(1)
+        rid, pid = topo.addr(T.cores[d], core)
+        a = 128 * slot(r, d)
+        arr = S["pa%d" % slot(r, d)]
+        g.wait_ge(S["hq%d" % t], 1)
+        g.remote_dma(T.lq[:, a:a + 128].bitcast(U8), T.hq[:, 128 * t:128 * t + 128].bitcast(U8),
+                     arr, S.lpg, pid, rid, eng(d))
+        g.remote_dma(T.lp[:, a:a + 128], T.hp[:, 128 * t:128 * t + 128], arr, S.lpg, pid, rid, eng(d))
+        if t == 3:
+            Y.wait_ge(S.v5, 1)
+            Y.dma_start(T.dd[:], T.bt[0:8, 0:32]).then_inc(S.dch, 16)
+            Y.dma_start(T.chs[0:1, 2 * r:2 * r + 2], T.bt[0:1, 10:12]).then_inc(S.chl, 16)
+            one = 1 << topo.engines(core, T.cores[others[0]])[0]
+            g.wait_ge(S.dch, 16)
+            g.remote_dma_fused([RemoteDMATransfer(
+                dst_ids=ids, dma_engine_mask=one, remote_sem=S.cha, srcs=[T.dd[:]],
+                dsts=[T.chd[128 * slot(r, d2):128 * slot(r, d2) + 128, :] for d2 in others])], local_sem=S.lch)
+
+    V.quantize_mx(T.pq[:], T.pp[:], T.pgt[:]).then_inc(S.qp, 1)
+    P.wait_ge(S.qw, 1)
+    P.wait_ge(S.qp, 1)
+    for j in range(2):
+        b = 512 * (1 + j)
+        P.matmul_mx(T.ps[:, b:b + 512], T.wq[:, 128 * j:128 * j + 128], T.wp[:, 128 * j:128 * j + 128],
+                    T.pq[:], T.pp[:], True, True).then_inc(S["om%d" % j], 1)
+        A.wait_ge(S["om%d" % j], 1)
+        A.activation(T.ow[:, 512 * j:512 * j + 512], T.ps[:, b:b + 512], COPY).then_inc(S["oc%d" % j], 1)
+    V.wait_ge(S.k5, 1)
+    for j in range(2):
+        V.tensor_scalar(T.offo[:, 4 * j:4 * j + 4], T.if64[:], T.bt[:, 10 + j:11 + j], 64.0,
+                        AluOpType.add, AluOpType.mult).then_inc(S.oo, 1)
+    V.wait_ge(S.oo, 2)
+    for j in range(2):
+        V.wait_ge(S["oc%d" % j], 1)
+        c = 64 * (j * NR + r)
+        V.tensor_copy(T.yb[:, c:c + 64], T.ow[:, 512 * j:512 * j + 512].indirect(T.offo[:, 4 * j:4 * j + 4])).then_inc(S["oy%d" % j], 1)
+        Y.wait_ge(S["oy%d" % j], 1)
+        Y.dma_start(T.y[:, c:c + 64], T.yb[:, c:c + 64]).then_inc(S.yst, 16)
+
+    banks = [(3, 4), (5, 6), (7, 0), (1, 2), (3, 4)]
+    for t in range(NO):
+        q = come[t]
+        s = slot(q, r)
+        P.wait_ge(S["pa%d" % s], 2 * count)
+        if t == 2:
+            P.wait_ge(S.v1, 1)
+        if t == 3:
+            P.wait_ge(S.oc0, 1)
+            P.wait_ge(S.oc1, 1)
+        if t == 4:
+            P.wait_ge(S.cp00, 1)
+            P.wait_ge(S.cp01, 1)
+        for j in range(2):
+            b = 512 * banks[t][j]
+            P.matmul_mx(T.ps[:, b:b + 128], T.wq[:, 128 * j:128 * j + 128], T.wp[:, 128 * j:128 * j + 128],
+                        T.lq[:, 128 * s:128 * s + 128], T.lp[:, 128 * s:128 * s + 128], True, True).then_inc(S["mm%d%d" % (t, j)], 1)
+        c = 64 * q
+        V.wait_ge(S["mm%d0" % t], 1)
+        V.tensor_copy(T.yb[:, c:c + 64], T.ps[:, 512 * banks[t][0]:512 * banks[t][0] + 64]).then_inc(S["cp%d0" % t], 1)
+        Y.wait_ge(S["cp%d0" % t], 1)
+        Y.dma_start(T.y[:, c:c + 64], T.yb[:, c:c + 64]).then_inc(S.yst, 16)
+        c = 64 * (NR + q)
+        A.wait_ge(S["mm%d1" % t], 1)
+        A.activation(T.yb[:, c:c + 64], T.ps[:, 512 * banks[t][1] + 64:512 * banks[t][1] + 128], COPY).then_inc(S["cp%d1" % t], 1)
+        A.wait_ge(S["cp%d1" % t], 1)
+        A.dma_start(T.y[:, c:c + 64], T.yb[:, c:c + 64]).then_inc(S.yst, 16)
+        if t == 3:
+            n = 16
+            Y.wait_ge(S.cha, NO)
+            if r > 0:
+                Y.dma_start(T.chs[0:1, 0:2 * r], T.chd[r - 1:128 * (r - 1) + r:128, :]).then_inc(S.chl, 16)
+                n += 16
+            if r < NR - 1:
+                Y.dma_start(T.chs[0:1, 2 * r + 2:12], T.chd[129 * r:512 + r + 1:128, :]).then_inc(S.chl, 16)
+                n += 16
+    V.wait_ge(S.chl, n)
+    for j in range(2):
+        V.tensor_copy(T.cho[0:1, 6 * j:6 * j + 6], T.chs[0:1, j:12:2]).then_inc(S.chv, 1)
+    Y.wait_ge(S.chv, 2)
+    Y.dma_start(T.ch[:], T.cho[0:1, :]).then_inc(S.chst, 16)
+
+    g.wait_ge(S.lg, 2 * count)
+    g.wait_ge(S.lpg, 2 * count * NO)
+    g.wait_ge(S.lch, 1)
+    Y.wait_ge(S.chst, 16)
+    Y.wait_ge(S.yst, 16 * 2 * NR)

@@ -5,6 +5,7 @@ U8 = dt.uint8
 COPY = ActivationFunctionType.Copy
 NR = 6
 NO = NR - 1
+NL = NR - 2
 
 SCRATCH = {
     "gt": ("sbuf", [128, 512], "bfloat16"),
@@ -19,12 +20,14 @@ SCRATCH = {
     "wp": ("sbuf", [128, 256], "uint8"),
     "pq": ("sbuf", [128, 512], "float8_e4m3fn_x4"),
     "pp": ("sbuf", [128, 512], "uint8"),
-    "hb": ("sbuf", [128, 2560], "bfloat16"),
-    "hq": ("sbuf", [128, 640], "float8_e4m3fn_x4"),
-    "hp": ("sbuf", [128, 640], "uint8"),
+    "eq": ("sbuf", [128, 512], "float8_e4m3fn_x4"),
+    "ep": ("sbuf", [128, 512], "uint8"),
+    "hb": ("sbuf", [128, 2048], "bfloat16"),
+    "hq": ("sbuf", [128, 512], "float8_e4m3fn_x4"),
+    "hp": ("sbuf", [128, 512], "uint8"),
     "lq": ("sbuf", [128, 640], "float8_e4m3fn_x4"),
     "lp": ("sbuf", [128, 640], "uint8"),
-    "ow": ("sbuf", [128, 1024], "float32"),
+    "ow": ("sbuf", [128, 2048], "float32"),
     "yb": ("sbuf", [128, 768], "float32"),
     "sc": ("sbuf", [128, 32], "float32"),
     "pm": ("sbuf", [128, 8], "float32"),
@@ -32,14 +35,15 @@ SCRATCH = {
     "zz": ("sbuf", [128, 40], "float32"),
     "bb": ("sbuf", [128, 64], "float32"),
     "bt": ("sbuf", [128, 32], "float32"),
+    "ce": ("sbuf", [128, 2], "float32"),
     "i0": ("sbuf", [128, 16], "int32"),
     "i1": ("sbuf", [128, 16], "int32"),
     "i2": ("sbuf", [128, 16], "int32"),
     "i3": ("sbuf", [128, 16], "float32"),
     "if256": ("sbuf", [128, 16], "float32"),
     "if64": ("sbuf", [128, 4], "float32"),
-    "off": ("sbuf", [128, 160], "uint16"),
-    "offo": ("sbuf", [128, 8], "uint16"),
+    "off": ("sbuf", [128, 128], "uint16"),
+    "offo": ("sbuf", [128, 16], "uint16"),
     "chs": ("sbuf", [128, 12], "float32"),
     "cho": ("sbuf", [128, 12], "float32"),
     "chd": ("dram", [640, 2], "float32"),
@@ -47,15 +51,12 @@ SCRATCH = {
     "ps": ("psum", [128, 4096], "float32"),
 }
 SEMAPHORES = (["gsl", "sml", "qwl", "pgl", "mg", "ms", "ml", "mz", "ii", "jj", "k2", "k3", "k4", "k5",
-               "cs", "qg", "qs", "qw", "qp", "sc", "v1", "v2", "v3", "v4", "v5", "oo", "go",
-               "gsa", "lg", "lpg", "lch", "dch", "cha", "chl", "chv", "chst", "yst", "kk"]
-              + ["of%d%d" % (t, j) for t in range(NO) for j in range(2)]
-              + ["gv%d" % t for t in range(NO)] + ["gz%d" % t for t in range(NO)]
-              + ["hq%d" % t for t in range(NO)]
+               "cs", "qg", "qs", "qw", "qp", "sc", "v1", "v2", "v3", "v4", "v5",
+               "gsa", "lg", "le", "ea", "lce", "cea", "lpg", "lch", "dch", "cha", "chl", "chv", "chst", "yst"]
+              + [n + "%d" % t for n in ("gv", "gz", "hq") for t in range(NL)]
               + ["pa%d" % t for t in range(NO)]
-              + ["mm%d%d" % (t, j) for t in range(NO) for j in range(2)]
-              + ["cp%d%d" % (t, j) for t in range(NO) for j in range(2)]
-              + ["om%d" % j for j in range(2)] + ["oc%d" % j for j in range(2)] + ["oy%d" % j for j in range(2)])
+              + [n + "%d%d" % (t, j) for n in ("of", "mm", "cp") for t in range(NL) for j in range(2)]
+              + [n + "%d" % t for n in ("om", "oc", "oo", "oy") for t in range(4)])
 
 
 def rank_program(g, core, T, topo):
@@ -66,8 +67,10 @@ def rank_program(g, core, T, topo):
     V, A, P, Y = g.vector, g.scalar, g.tensor, g.sync
     others = [q for q in range(NR) if q != r]
     slot = lambda q, at: q - (q > at)
-    order = [(r + 1 + t) % NR for t in range(NO)]
-    come = [(r - 1 - t) % NR for t in range(NO)]
+    order = [(r + 1 + t) % NR for t in range(NL)]
+    come = [(r - 1 - t) % NR for t in range(NL)]
+    eto = (r + NO) % NR
+    efrom = (r + 1) % NR
     eng = lambda d: topo.mask(core, T.cores[d])
     allmask = eng(others[0])
     for d in others:
@@ -80,9 +83,9 @@ def rank_program(g, core, T, topo):
 
     Y.dma_start(T.gt[:, 0:8], T.gs[:, 0:8]).then_inc(S.gsl, 16)
     A.dma_start(T.st[:, 0:32], T.sm[:, 0:32]).then_inc(S.sml, 16)
-    A.dma_start(T.wt[:], T.qw[:]).then_inc(S.qwl, 16)
     for m in range(8):
         (Y if m % 2 == 0 else A).dma_start(T.pgt[:, 256 * m:256 * m + 256], T.pg[128 * m:128 * m + 128, :]).then_inc(S.pgl, 16)
+    A.dma_start(T.wt[:], T.qw[:]).then_inc(S.qwl, 16)
 
     g.iota(T.i0[:], [[0, 16]], 0, 1).then_inc(S.ii, 1)
     g.iota(T.i1[:], [[16, 16]], 0, 0).then_inc(S.jj, 1)
@@ -97,10 +100,12 @@ def rank_program(g, core, T, topo):
     g.wait_ge(S.qg, 1)
     ids = [did(d) for d in others]
     at = [6 + 2 * slot(r, d) for d in others]
-    g.remote_dma_fused([RemoteDMATransfer(dst_ids=ids, dma_engine_mask=allmask, remote_sem=S.gsa,
+    half = [e for e in range(allmask.bit_length()) if allmask >> e & 1]
+    half = [sum(1 << e for e in half[:count // 2]), sum(1 << e for e in half[count // 2:])]
+    g.remote_dma_fused([RemoteDMATransfer(dst_ids=ids, dma_engine_mask=half[0], remote_sem=S.gsa,
                                           srcs=[T.gq[:, 16:18].bitcast(U8)],
                                           dsts=[T.gq[:, a:a + 2].bitcast(U8) for a in at])], local_sem=S.lg)
-    g.remote_dma_fused([RemoteDMATransfer(dst_ids=ids, dma_engine_mask=allmask, remote_sem=S.gsa,
+    g.remote_dma_fused([RemoteDMATransfer(dst_ids=ids, dma_engine_mask=half[1], remote_sem=S.gsa,
                                           srcs=[T.gp[:, 16:18]],
                                           dsts=[T.gp[:, a:a + 2] for a in at])], local_sem=S.lg)
 
@@ -119,12 +124,19 @@ def rank_program(g, core, T, topo):
         V.tensor_copy(T.st[:, 128 * a:128 * a + 32], T.st[:, 0:32]).then_inc(S.cs, 1)
     V.wait_ge(S.cs, 3)
     V.quantize_mx(T.sq[:], T.sp[:], T.st[:]).then_inc(S.qs, 1)
+    V.wait_ge(S.pgl, 128)
+    V.quantize_mx(T.pq[:], T.pp[:], T.pgt[:]).then_inc(S.qp, 1)
     V.wait_ge(S.qwl, 16)
     V.quantize_mx(T.wq[:], T.wp[:], T.wt[:]).then_inc(S.qw, 1)
 
+    rid, pid = topo.addr(T.cores[eto], core)
+    g.wait_ge(S.qp, 1)
+    g.remote_dma(T["eq"][:].bitcast(U8), T.pq[:].bitcast(U8), S.ea, S.le, pid, rid, eng(eto))
+    g.remote_dma(T["ep"][:], T.pp[:], S.ea, S.le, pid, rid, eng(eto))
+
     P.wait_ge(S.qs, 1)
     P.wait_ge(S.qg, 1)
-    P.wait_ge(S.gsa, 2 * count * NO)
+    P.wait_ge(S.gsa, count * NO)
     P.matmul_mx(T.ps[:, 0:138], T.sq[:], T.sp[:], T.gq[:, 6:144], T.gp[:, 6:144], True, True).then_inc(S.sc, 1)
 
     V.wait_ge(S.sc, 1)
@@ -142,10 +154,16 @@ def rank_program(g, core, T, topo):
     V.wait_ge(S.v4, 1)
     V.transpose(T.bt[:], T.bb[:, 32:64]).then_inc(S.v5, 1)
 
+    Y.wait_ge(S.v5, 1)
+    Y.dma_start(T.dd[:], T.bt[0:8, 0:32]).then_inc(S.dch, 16)
+    Y.dma_start(T.chs[0:1, 2 * r:2 * r + 2], T.bt[0:1, 10:12]).then_inc(S.chl, 16)
+    g.wait_ge(S.v5, 1)
+    c = 2 * slot(eto, r)
+    g.remote_dma(T.ce[:], T.bt[:, c:c + 2], S.cea, S.lce, pid, rid, eng(eto))
+
     V.wait_ge(S.k4, 1)
     V.wait_ge(S.v5, 1)
     win = T.pgt[:, 0:2048]
-    both = (3,)
 
     def offsets(t):
         for j in (1, 0):
@@ -155,29 +173,23 @@ def rank_program(g, core, T, topo):
                             AluOpType.add, AluOpType.mult).then_inc(S["of%d%d" % (t, j)], 1)
 
     offsets(0)
-    for t in range(NO):
-        d = order[t]
+    for t in range(NL):
         k, h = 32 * t, 512 * t
         if t == 0:
             A.wait_ge(S.pgl, 128)
-            V.wait_ge(S.pgl, 128)
         A.wait_ge(S["of%d1" % t], 1)
-        if t in both:
-            A.wait_ge(S["of%d0" % t], 1)
-            A.activation(T.hb[:, h:h + 512], win.indirect(T.off[:, k:k + 32]), COPY).then_inc(S["gz%d" % t], 1)
-        else:
-            A.activation(T.hb[:, h + 256:h + 512], win.indirect(T.off[:, k + 16:k + 32]), COPY).then_inc(S["gz%d" % t], 1)
-            V.wait_ge(S["of%d0" % t], 1)
-            V.tensor_copy(T.hb[:, h:h + 256], win.indirect(T.off[:, k:k + 16])).then_inc(S["gv%d" % t], 1)
-        if 0 < t < NO - 1:
+        A.activation(T.hb[:, h + 256:h + 512], win.indirect(T.off[:, k + 16:k + 32]), COPY).then_inc(S["gz%d" % t], 1)
+        V.wait_ge(S["of%d0" % t], 1)
+        V.tensor_copy(T.hb[:, h:h + 256], win.indirect(T.off[:, k:k + 16])).then_inc(S["gv%d" % t], 1)
+        if 0 < t < NL - 1:
             offsets(t + 1)
-        if t not in both:
-            V.wait_ge(S["gv%d" % t], 1)
+        V.wait_ge(S["gv%d" % t], 1)
         V.wait_ge(S["gz%d" % t], 1)
         V.quantize_mx(T.hq[:, 128 * t:128 * t + 128], T.hp[:, 128 * t:128 * t + 128],
                       T.hb[:, h:h + 512]).then_inc(S["hq%d" % t], 1)
         if t == 0:
             offsets(1)
+        d = order[t]
         rid, pid = topo.addr(T.cores[d], core)
         a = 128 * slot(r, d)
         arr = S["pa%d" % slot(r, d)]
@@ -185,81 +197,98 @@ def rank_program(g, core, T, topo):
         g.remote_dma(T.lq[:, a:a + 128].bitcast(U8), T.hq[:, 128 * t:128 * t + 128].bitcast(U8),
                      arr, S.lpg, pid, rid, eng(d))
         g.remote_dma(T.lp[:, a:a + 128], T.hp[:, 128 * t:128 * t + 128], arr, S.lpg, pid, rid, eng(d))
-        if t == 3:
-            Y.wait_ge(S.v5, 1)
-            Y.dma_start(T.dd[:], T.bt[0:8, 0:32]).then_inc(S.dch, 16)
-            Y.dma_start(T.chs[0:1, 2 * r:2 * r + 2], T.bt[0:1, 10:12]).then_inc(S.chl, 16)
+        if t == 2:
             one = 1 << topo.engines(core, T.cores[others[0]])[0]
             g.wait_ge(S.dch, 16)
             g.remote_dma_fused([RemoteDMATransfer(
-                dst_ids=ids, dma_engine_mask=one, remote_sem=S.cha, srcs=[T.dd[:]],
-                dsts=[T.chd[128 * slot(r, d2):128 * slot(r, d2) + 128, :] for d2 in others])], local_sem=S.lch)
+                dst_ids=[did(x) for x in order], dma_engine_mask=one, remote_sem=S.cha, srcs=[T.dd[:]],
+                dsts=[T.chd[128 * slot(r, x):128 * slot(r, x) + 128, :] for x in order])], local_sem=S.lch)
 
-    V.quantize_mx(T.pq[:], T.pp[:], T.pgt[:]).then_inc(S.qp, 1)
+    n = 32
+    Y.wait_ge(S.cea, count)
+    Y.dma_start(T.chs[0:1, 2 * efrom:2 * efrom + 2], T.ce[0:1, :]).then_inc(S.chl, 16)
+    Y.wait_ge(S.cha, NL)
+    for qs in ([q for q in range(r) if q != efrom], [q for q in range(r + 1, NR) if q != efrom]):
+        if qs:
+            lo, hi, at = slot(qs[0], r), slot(qs[-1], r), slot(r, qs[0])
+            Y.dma_start(T.chs[0:1, 2 * qs[0]:2 * qs[-1] + 2], T.chd[128 * lo + at:128 * hi + at + 1:128, :]).then_inc(S.chl, 16)
+            n += 16
+
     P.wait_ge(S.qw, 1)
     P.wait_ge(S.qp, 1)
-    for j in range(2):
-        b = 512 * (1 + j)
+    for i in range(4):
+        j = i % 2
+        b = 512 * (1 + i)
+        if i == 2:
+            P.wait_ge(S.ea, 2 * count)
+        mq, mp = (T.pq, T.pp) if i < 2 else (T["eq"], T["ep"])
         P.matmul_mx(T.ps[:, b:b + 512], T.wq[:, 128 * j:128 * j + 128], T.wp[:, 128 * j:128 * j + 128],
-                    T.pq[:], T.pp[:], True, True).then_inc(S["om%d" % j], 1)
-        A.wait_ge(S["om%d" % j], 1)
-        A.activation(T.ow[:, 512 * j:512 * j + 512], T.ps[:, b:b + 512], COPY).then_inc(S["oc%d" % j], 1)
-    V.wait_ge(S.k5, 1)
-    for j in range(2):
-        V.tensor_scalar(T.offo[:, 4 * j:4 * j + 4], T.if64[:], T.bt[:, 10 + j:11 + j], 64.0,
-                        AluOpType.add, AluOpType.mult).then_inc(S.oo, 1)
-    V.wait_ge(S.oo, 2)
-    for j in range(2):
-        V.wait_ge(S["oc%d" % j], 1)
-        c = 64 * (j * NR + r)
-        V.tensor_copy(T.yb[:, c:c + 64], T.ow[:, 512 * j:512 * j + 512].indirect(T.offo[:, 4 * j:4 * j + 4])).then_inc(S["oy%d" % j], 1)
-        Y.wait_ge(S["oy%d" % j], 1)
+                    mq[:], mp[:], True, True).then_inc(S["om%d" % i], 1)
+        if i != 2:
+            A.wait_ge(S["om%d" % i], 1)
+            A.activation(T.ow[:, 512 * i:512 * i + 512], T.ps[:, b:b + 512], COPY).then_inc(S["oc%d" % i], 1)
+
+    def listed(i):
+        V.wait_ge(S["oo%d" % i], 1)
+        V.wait_ge(S["oc%d" % i], 1)
+        c = 64 * (i % 2 * NR + (r if i < 2 else efrom))
+        V.tensor_copy(T.yb[:, c:c + 64], T.ow[:, 512 * i:512 * i + 512].indirect(T.offo[:, 4 * i:4 * i + 4])).then_inc(S["oy%d" % i], 1)
+        Y.wait_ge(S["oy%d" % i], 1)
         Y.dma_start(T.y[:, c:c + 64], T.yb[:, c:c + 64]).then_inc(S.yst, 16)
 
-    banks = [(3, 4), (5, 6), (7, 0), (1, 2), (3, 4)]
-    for t in range(NO):
+    V.wait_ge(S.k5, 1)
+    for i in range(4):
+        if i == 2:
+            V.wait_ge(S.cea, count)
+        src = T.bt[:, 10 + i:11 + i] if i < 2 else T.ce[:, i - 2:i - 1]
+        V.tensor_scalar(T.offo[:, 4 * i:4 * i + 4], T.if64[:], src, 64.0,
+                        AluOpType.add, AluOpType.mult).then_inc(S["oo%d" % i], 1)
+    V.wait_ge(S.om2, 1)
+    V.tensor_copy(T.ow[:, 1024:1536], T.ps[:, 1536:2048]).then_inc(S.oc2, 1)
+
+    banks = [(5, 6), (7, 0), (1, 2), (3, 4)]
+    for t in range(NL):
+        bank = banks[t]
         q = come[t]
-        s = slot(q, r)
-        P.wait_ge(S["pa%d" % s], 2 * count)
-        if t == 2:
+        lo = 128 * slot(q, r)
+        P.wait_ge(S["pa%d" % slot(q, r)], 2 * count)
+        if t == 1:
             P.wait_ge(S.v1, 1)
-        if t == 3:
-            P.wait_ge(S.oc0, 1)
-            P.wait_ge(S.oc1, 1)
-        if t == 4:
-            P.wait_ge(S.cp00, 1)
-            P.wait_ge(S.cp01, 1)
+        if t >= 2:
+            P.wait_ge(S["oc%d" % (2 * t - 4)], 1)
+            P.wait_ge(S["oc%d" % (2 * t - 3)], 1)
         for j in range(2):
-            b = 512 * banks[t][j]
-            P.matmul_mx(T.ps[:, b:b + 128], T.wq[:, 128 * j:128 * j + 128], T.wp[:, 128 * j:128 * j + 128],
-                        T.lq[:, 128 * s:128 * s + 128], T.lp[:, 128 * s:128 * s + 128], True, True).then_inc(S["mm%d%d" % (t, j)], 1)
+            P.matmul_mx(T.ps[:, 512 * bank[j]:512 * bank[j] + 128], T.wq[:, 128 * j:128 * j + 128],
+                        T.wp[:, 128 * j:128 * j + 128], T.lq[:, lo:lo + 128], T.lp[:, lo:lo + 128],
+                        True, True).then_inc(S["mm%d%d" % (t, j)], 1)
         c = 64 * q
+        b = 512 * bank[0]
         V.wait_ge(S["mm%d0" % t], 1)
-        V.tensor_copy(T.yb[:, c:c + 64], T.ps[:, 512 * banks[t][0]:512 * banks[t][0] + 64]).then_inc(S["cp%d0" % t], 1)
+        V.tensor_copy(T.yb[:, c:c + 64], T.ps[:, b:b + 64]).then_inc(S["cp%d0" % t], 1)
         Y.wait_ge(S["cp%d0" % t], 1)
         Y.dma_start(T.y[:, c:c + 64], T.yb[:, c:c + 64]).then_inc(S.yst, 16)
         c = 64 * (NR + q)
+        b = 512 * bank[1] + 64
         A.wait_ge(S["mm%d1" % t], 1)
-        A.activation(T.yb[:, c:c + 64], T.ps[:, 512 * banks[t][1] + 64:512 * banks[t][1] + 128], COPY).then_inc(S["cp%d1" % t], 1)
+        A.activation(T.yb[:, c:c + 64], T.ps[:, b:b + 64], COPY).then_inc(S["cp%d1" % t], 1)
         A.wait_ge(S["cp%d1" % t], 1)
         A.dma_start(T.y[:, c:c + 64], T.yb[:, c:c + 64]).then_inc(S.yst, 16)
-        if t == 3:
-            n = 16
-            Y.wait_ge(S.cha, NO)
-            if r > 0:
-                Y.dma_start(T.chs[0:1, 0:2 * r], T.chd[r - 1:128 * (r - 1) + r:128, :]).then_inc(S.chl, 16)
-                n += 16
-            if r < NR - 1:
-                Y.dma_start(T.chs[0:1, 2 * r + 2:12], T.chd[129 * r:512 + r + 1:128, :]).then_inc(S.chl, 16)
-                n += 16
-    V.wait_ge(S.chl, n)
-    for j in range(2):
-        V.tensor_copy(T.cho[0:1, 6 * j:6 * j + 6], T.chs[0:1, j:12:2]).then_inc(S.chv, 1)
-    Y.wait_ge(S.chv, 2)
-    Y.dma_start(T.ch[:], T.cho[0:1, :]).then_inc(S.chst, 16)
+        if t == 0:
+            listed(0)
+            listed(1)
+            listed(2)
+            listed(3)
+        if t == 1:
+            V.wait_ge(S.chl, n)
+            for j in range(2):
+                V.tensor_copy(T.cho[0:1, 6 * j:6 * j + 6], T.chs[0:1, j:12:2]).then_inc(S.chv, 1)
+            Y.wait_ge(S.chv, 2)
+            Y.dma_start(T.ch[:], T.cho[0:1, :]).then_inc(S.chst, 16)
 
-    g.wait_ge(S.lg, 2 * count)
-    g.wait_ge(S.lpg, 2 * count * NO)
+    g.wait_ge(S.lg, count)
+    g.wait_ge(S.le, 2 * count)
+    g.wait_ge(S.lce, count)
+    g.wait_ge(S.lpg, 2 * count * NL)
     g.wait_ge(S.lch, 1)
     Y.wait_ge(S.chst, 16)
     Y.wait_ge(S.yst, 16 * 2 * NR)

from concourse.bass import DstId, RemoteDMATransfer
from concourse.mybir import dt, AluOpType, ActivationFunctionType

U8 = dt.uint8
COPY = ActivationFunctionType.Copy
NR = 6
NO = NR - 1
NL = NR - 2

SCRATCH = {
    "gt": ("sbuf", [128, 512], "bfloat16"),
    "st": ("sbuf", [128, 512], "bfloat16"),
    "pgt": ("sbuf", [128, 2048], "bfloat16"),
    "wt": ("sbuf", [128, 1024], "bfloat16"),
    "gq": ("sbuf", [128, 144], "float8_e4m3fn_x4"),
    "gp": ("sbuf", [128, 144], "uint8"),
    "sq": ("sbuf", [128, 128], "float8_e4m3fn_x4"),
    "sp": ("sbuf", [128, 128], "uint8"),
    "wq": ("sbuf", [128, 256], "float8_e4m3fn_x4"),
    "wp": ("sbuf", [128, 256], "uint8"),
    "pq": ("sbuf", [128, 512], "float8_e4m3fn_x4"),
    "pp": ("sbuf", [128, 512], "uint8"),
    "eq": ("sbuf", [128, 512], "float8_e4m3fn_x4"),
    "ep": ("sbuf", [128, 512], "uint8"),
    "hb": ("sbuf", [128, 2048], "bfloat16"),
    "hq": ("sbuf", [128, 512], "float8_e4m3fn_x4"),
    "hp": ("sbuf", [128, 512], "uint8"),
    "lq": ("sbuf", [128, 640], "float8_e4m3fn_x4"),
    "lp": ("sbuf", [128, 640], "uint8"),
    "ow": ("sbuf", [128, 2048], "float32"),
    "yb": ("sbuf", [128, 768], "float32"),
    "sc": ("sbuf", [128, 32], "float32"),
    "pm": ("sbuf", [128, 8], "float32"),
    "lt": ("sbuf", [128, 64], "float32"),
    "zz": ("sbuf", [128, 40], "float32"),
    "bb": ("sbuf", [128, 64], "float32"),
    "bt": ("sbuf", [128, 32], "float32"),
    "ce": ("sbuf", [128, 2], "float32"),
    "i0": ("sbuf", [128, 16], "int32"),
    "i1": ("sbuf", [128, 16], "int32"),
    "i2": ("sbuf", [128, 16], "int32"),
    "i3": ("sbuf", [128, 16], "float32"),
    "if256": ("sbuf", [128, 16], "float32"),
    "if64": ("sbuf", [128, 4], "float32"),
    "off": ("sbuf", [128, 128], "uint16"),
    "offo": ("sbuf", [128, 16], "uint16"),
    "chs": ("sbuf", [128, 12], "float32"),
    "cho": ("sbuf", [128, 12], "float32"),
    "chd": ("dram", [640, 2], "float32"),
    "dd": ("dram", [128, 2], "float32"),
    "ps": ("psum", [128, 4096], "float32"),
}
SEMAPHORES = (["gsl", "sml", "qwl", "pgl", "mg", "ms", "ml", "mz", "ii", "jj", "k2", "k3", "k4", "k5",
               "cs", "qg", "qs", "qw", "qp", "sc", "v1", "v2", "v3", "v4", "v5",
               "gsa", "lg", "le", "ea", "lce", "cea", "lpg", "lch", "dch", "cha", "chl", "chv", "chst", "yst"]
              + [n + "%d" % t for n in ("gv", "gz", "hq") for t in range(NL)]
              + ["pa%d" % t for t in range(NO)]
              + [n + "%d%d" % (t, j) for n in ("of", "mm", "cp") for t in range(NL) for j in range(2)]
              + [n + "%d" % t for n in ("om", "oc", "oo", "oy") for t in range(4)])


def rank_program(g, core, T, topo):
    r = T.rank_of(core)
    if r is None:
        return
    S = T.sem
    V, A, P, Y = g.vector, g.scalar, g.tensor, g.sync
    others = [q for q in range(NR) if q != r]
    slot = lambda q, at: q - (q > at)
    order = [(r + 1 + t) % NR for t in range(NL)]
    come = [(r - 1 - t) % NR for t in range(NL)]
    eto = (r + NO) % NR
    efrom = (r + 1) % NR
    eng = lambda d: topo.mask(core, T.cores[d])
    allmask = eng(others[0])
    for d in others:
        allmask &= eng(d)
    count = bin(allmask).count("1")

    def did(d):
        rid, pid = topo.addr(T.cores[d], core)
        return DstId(rid=rid, pnc=pid)

    Y.dma_start(T.gt[:, 0:8], T.gs[:, 0:8]).then_inc(S.gsl, 16)
    A.dma_start(T.st[:, 0:32], T.sm[:, 0:32]).then_inc(S.sml, 16)
    for m in range(8):
        (Y if m % 2 == 0 else A).dma_start(T.pgt[:, 256 * m:256 * m + 256], T.pg[128 * m:128 * m + 128, :]).then_inc(S.pgl, 16)
    A.dma_start(T.wt[:], T.qw[:]).then_inc(S.qwl, 16)

    g.iota(T.i0[:], [[0, 16]], 0, 1).then_inc(S.ii, 1)
    g.iota(T.i1[:], [[16, 16]], 0, 0).then_inc(S.jj, 1)
    V.memset(T.gt[:, 8:512], 0.0).then_inc(S.mg, 1)
    V.memset(T.st[:, 32:512], 0.0).then_inc(S.ms, 1)
    V.memset(T.lt[:, 32:64], 0.0).then_inc(S.ml, 1)
    V.memset(T.zz[:], 0.0).then_inc(S.mz, 1)

    V.wait_ge(S.mg, 1)
    V.wait_ge(S.gsl, 16)
    V.quantize_mx(T.gq[:, 16:144], T.gp[:, 16:144], T.gt[:]).then_inc(S.qg, 1)
    g.wait_ge(S.qg, 1)
    ids = [did(d) for d in others]
    at = [6 + 2 * slot(r, d) for d in others]
    half = [e for e in range(allmask.bit_length()) if allmask >> e & 1]
    half = [sum(1 << e for e in half[:count // 2]), sum(1 << e for e in half[count // 2:])]
    g.remote_dma_fused([RemoteDMATransfer(dst_ids=ids, dma_engine_mask=half[0], remote_sem=S.gsa,
                                          srcs=[T.gq[:, 16:18].bitcast(U8)],
                                          dsts=[T.gq[:, a:a + 2].bitcast(U8) for a in at])], local_sem=S.lg)
    g.remote_dma_fused([RemoteDMATransfer(dst_ids=ids, dma_engine_mask=half[1], remote_sem=S.gsa,
                                          srcs=[T.gp[:, 16:18]],
                                          dsts=[T.gp[:, a:a + 2] for a in at])], local_sem=S.lg)

    V.wait_ge(S.ii, 1)
    V.tensor_scalar(T.i2[:], T.i0[:], 15, None, AluOpType.bitwise_and).then_inc(S.k2, 1)
    V.wait_ge(S.k2, 1)
    V.wait_ge(S.jj, 1)
    V.tensor_tensor(T.i3[:], T.i2[:], T.i1[:], AluOpType.add).then_inc(S.k3, 1)
    V.wait_ge(S.k3, 1)
    V.tensor_scalar(T.if256[:], T.i3[:], 1.0 / 256, None, AluOpType.mult).then_inc(S.k4, 1)
    V.tensor_scalar(T.if64[:], T.i3[:, 0:4], 1.0 / 64, None, AluOpType.mult).then_inc(S.k5, 1)

    V.wait_ge(S.ms, 1)
    V.wait_ge(S.sml, 16)
    for a in range(1, 4):
        V.tensor_copy(T.st[:, 128 * a:128 * a + 32], T.st[:, 0:32]).then_inc(S.cs, 1)
    V.wait_ge(S.cs, 3)
    V.quantize_mx(T.sq[:], T.sp[:], T.st[:]).then_inc(S.qs, 1)
    V.wait_ge(S.pgl, 128)
    V.quantize_mx(T.pq[:], T.pp[:], T.pgt[:]).then_inc(S.qp, 1)
    V.wait_ge(S.qwl, 16)
    V.quantize_mx(T.wq[:], T.wp[:], T.wt[:]).then_inc(S.qw, 1)

    rid, pid = topo.addr(T.cores[eto], core)
    g.wait_ge(S.qp, 1)
    g.remote_dma(T["eq"][:].bitcast(U8), T.pq[:].bitcast(U8), S.ea, S.le, pid, rid, eng(eto))
    g.remote_dma(T["ep"][:], T.pp[:], S.ea, S.le, pid, rid, eng(eto))

    P.wait_ge(S.qs, 1)
    P.wait_ge(S.qg, 1)
    P.wait_ge(S.gsa, count * NO)
    P.matmul_mx(T.ps[:, 0:138], T.sq[:], T.sp[:], T.gq[:, 6:144], T.gp[:, 6:144], True, True).then_inc(S.sc, 1)

    V.wait_ge(S.sc, 1)
    V.transpose(T["sc"][:], T.ps[:, 0:32]).then_inc(S.v1, 1)
    V.wait_ge(S.v1, 1)
    V.tensor_tensor_scan(T["pm"][:], T["sc"][:, 0:8], T["sc"][:, 0:8], T["sc"][:, 0:1],
                         AluOpType.max, AluOpType.max).then_inc(S.v2, 1)
    V.wait_ge(S.v2, 1)
    V.tensor_scalar(T["lt"][:, 24:32], T["pm"][:], T["pm"][:, 7:8], None, AluOpType.is_lt).then_inc(S.v3, 1)
    V.wait_ge(S.ml, 1)
    V.wait_ge(S.mz, 1)
    V.wait_ge(S.v3, 1)
    V.tensor_tensor_scan(T.bb[:, 24:64], T["lt"][:, 24:64], T.zz[:], 0.0,
                         AluOpType.add, AluOpType.add).then_inc(S.v4, 1)
    V.wait_ge(S.v4, 1)
    V.transpose(T.bt[:], T.bb[:, 32:64]).then_inc(S.v5, 1)

    Y.wait_ge(S.v5, 1)
    Y.dma_start(T.dd[:], T.bt[0:8, 0:32]).then_inc(S.dch, 16)
    Y.dma_start(T.chs[0:1, 2 * r:2 * r + 2], T.bt[0:1, 10:12]).then_inc(S.chl, 16)
    g.wait_ge(S.v5, 1)
    c = 2 * slot(eto, r)
    g.remote_dma(T.ce[:], T.bt[:, c:c + 2], S.cea, S.lce, pid, rid, eng(eto))

    V.wait_ge(S.k4, 1)
    V.wait_ge(S.v5, 1)
    win = T.pgt[:, 0:2048]

    def offsets(t):
        for j in (1, 0):
            c = 2 * slot(order[t], r) + j
            k = 32 * t + 16 * j
            V.tensor_scalar(T.off[:, k:k + 16], T.if256[:], T.bt[:, c:c + 1], 256.0,
                            AluOpType.add, AluOpType.mult).then_inc(S["of%d%d" % (t, j)], 1)

    offsets(0)
    for t in range(NL):
        k, h = 32 * t, 512 * t
        if t == 0:
            A.wait_ge(S.pgl, 128)
        A.wait_ge(S["of%d1" % t], 1)
        A.activation(T.hb[:, h + 256:h + 512], win.indirect(T.off[:, k + 16:k + 32]), COPY).then_inc(S["gz%d" % t], 1)
        V.wait_ge(S["of%d0" % t], 1)
        V.tensor_copy(T.hb[:, h:h + 256], win.indirect(T.off[:, k:k + 16])).then_inc(S["gv%d" % t], 1)
        if 0 < t < NL - 1:
            offsets(t + 1)
        V.wait_ge(S["gv%d" % t], 1)
        V.wait_ge(S["gz%d" % t], 1)
        V.quantize_mx(T.hq[:, 128 * t:128 * t + 128], T.hp[:, 128 * t:128 * t + 128],
                      T.hb[:, h:h + 512]).then_inc(S["hq%d" % t], 1)
        if t == 0:
            offsets(1)
        d = order[t]
        rid, pid = topo.addr(T.cores[d], core)
        a = 128 * slot(r, d)
        arr = S["pa%d" % slot(r, d)]
        g.wait_ge(S["hq%d" % t], 1)
        g.remote_dma(T.lq[:, a:a + 128].bitcast(U8), T.hq[:, 128 * t:128 * t + 128].bitcast(U8),
                     arr, S.lpg, pid, rid, eng(d))
        g.remote_dma(T.lp[:, a:a + 128], T.hp[:, 128 * t:128 * t + 128], arr, S.lpg, pid, rid, eng(d))
        if t == 2:
            one = 1 << topo.engines(core, T.cores[others[0]])[0]
            g.wait_ge(S.dch, 16)
            g.remote_dma_fused([RemoteDMATransfer(
                dst_ids=[did(x) for x in order], dma_engine_mask=one, remote_sem=S.cha, srcs=[T.dd[:]],
                dsts=[T.chd[128 * slot(r, x):128 * slot(r, x) + 128, :] for x in order])], local_sem=S.lch)

    n = 32
    Y.wait_ge(S.cea, count)
    Y.dma_start(T.chs[0:1, 2 * efrom:2 * efrom + 2], T.ce[0:1, :]).then_inc(S.chl, 16)
    Y.wait_ge(S.cha, NL)
    for qs in ([q for q in range(r) if q != efrom], [q for q in range(r + 1, NR) if q != efrom]):
        if qs:
            lo, hi, at = slot(qs[0], r), slot(qs[-1], r), slot(r, qs[0])
            Y.dma_start(T.chs[0:1, 2 * qs[0]:2 * qs[-1] + 2], T.chd[128 * lo + at:128 * hi + at + 1:128, :]).then_inc(S.chl, 16)
            n += 16

    P.wait_ge(S.qw, 1)
    P.wait_ge(S.qp, 1)
    for i in range(4):
        j = i % 2
        b = 512 * (1 + i)
        if i == 2:
            P.wait_ge(S.ea, 2 * count)
        mq, mp = (T.pq, T.pp) if i < 2 else (T["eq"], T["ep"])
        P.matmul_mx(T.ps[:, b:b + 512], T.wq[:, 128 * j:128 * j + 128], T.wp[:, 128 * j:128 * j + 128],
                    mq[:], mp[:], True, True).then_inc(S["om%d" % i], 1)
        if i != 2:
            A.wait_ge(S["om%d" % i], 1)
            A.activation(T.ow[:, 512 * i:512 * i + 512], T.ps[:, b:b + 512], COPY).then_inc(S["oc%d" % i], 1)

    def listed(i):
        V.wait_ge(S["oo%d" % i], 1)
        V.wait_ge(S["oc%d" % i], 1)
        c = 64 * (i % 2 * NR + (r if i < 2 else efrom))
        V.tensor_copy(T.yb[:, c:c + 64], T.ow[:, 512 * i:512 * i + 512].indirect(T.offo[:, 4 * i:4 * i + 4])).then_inc(S["oy%d" % i], 1)
        Y.wait_ge(S["oy%d" % i], 1)
        Y.dma_start(T.y[:, c:c + 64], T.yb[:, c:c + 64]).then_inc(S.yst, 16)

    V.wait_ge(S.k5, 1)
    for i in range(4):
        if i == 2:
            V.wait_ge(S.cea, count)
        src = T.bt[:, 10 + i:11 + i] if i < 2 else T.ce[:, i - 2:i - 1]
        V.tensor_scalar(T.offo[:, 4 * i:4 * i + 4], T.if64[:], src, 64.0,
                        AluOpType.add, AluOpType.mult).then_inc(S["oo%d" % i], 1)
    V.wait_ge(S.om2, 1)
    V.tensor_copy(T.ow[:, 1024:1536], T.ps[:, 1536:2048]).then_inc(S.oc2, 1)

    banks = [(5, 6), (7, 0), (1, 2), (3, 4)]
    for t in range(NL):
        bank = banks[t]
        q = come[t]
        lo = 128 * slot(q, r)
        P.wait_ge(S["pa%d" % slot(q, r)], 2 * count)
        if t == 1:
            P.wait_ge(S.v1, 1)
        if t >= 2:
            P.wait_ge(S["oc%d" % (2 * t - 4)], 1)
            P.wait_ge(S["oc%d" % (2 * t - 3)], 1)
        for j in range(2):
            P.matmul_mx(T.ps[:, 512 * bank[j]:512 * bank[j] + 128], T.wq[:, 128 * j:128 * j + 128],
                        T.wp[:, 128 * j:128 * j + 128], T.lq[:, lo:lo + 128], T.lp[:, lo:lo + 128],
                        True, True).then_inc(S["mm%d%d" % (t, j)], 1)
        c = 64 * q
        b = 512 * bank[0]
        V.wait_ge(S["mm%d0" % t], 1)
        V.tensor_copy(T.yb[:, c:c + 64], T.ps[:, b:b + 64]).then_inc(S["cp%d0" % t], 1)
        Y.wait_ge(S["cp%d0" % t], 1)
        Y.dma_start(T.y[:, c:c + 64], T.yb[:, c:c + 64]).then_inc(S.yst, 16)
        c = 64 * (NR + q)
        b = 512 * bank[1] + 64
        A.wait_ge(S["mm%d1" % t], 1)
        A.activation(T.yb[:, c:c + 64], T.ps[:, b:b + 64], COPY).then_inc(S["cp%d1" % t], 1)
        A.wait_ge(S["cp%d1" % t], 1)
        A.dma_start(T.y[:, c:c + 64], T.yb[:, c:c + 64]).then_inc(S.yst, 16)
        if t == 0:
            listed(0)
            listed(1)
            listed(2)
            listed(3)
        if t == 1:
            V.wait_ge(S.chl, n)
            for j in range(2):
                V.tensor_copy(T.cho[0:1, 6 * j:6 * j + 6], T.chs[0:1, j:12:2]).then_inc(S.chv, 1)
            Y.wait_ge(S.chv, 2)
            Y.dma_start(T.ch[:], T.cho[0:1, :]).then_inc(S.chst, 16)

    g.wait_ge(S.lg, count)
    g.wait_ge(S.le, 2 * count)
    g.wait_ge(S.lce, count)
    g.wait_ge(S.lpg, 2 * count * NL)
    g.wait_ge(S.lch, 1)
    Y.wait_ge(S.chst, 16)
    Y.wait_ge(S.yst, 16 * 2 * NR)
